import numpy as np, ml_dtypes
CORES = [76,84,92,100,108,116,124]
N = 7
KB, QP = 2, 32
ROOT = 3
def setup_inputs(rng):
    q = rng.standard_normal((N, 128, QP), dtype=np.float32) / 4; k = rng.standard_normal((N, 128, KB * 128), dtype=np.float32)
    a = 2 * np.pi * rng.random((N, QP)); s = 400 * rng.random((N, QP)) ** 1.5; q[:, 0, :] = s * np.cos(a); q[:, 1, :] = s * np.sin(a); q[:, 2, :] = 150 * rng.standard_normal((N, QP)); k[:, 2, :] = 1 + k[:, 2, :] / 50
    a = (2 * np.pi * rng.random() + np.pi / 2 * (rng.permutation(N).reshape(N, 1, 1) + 0.5) / N - 0.5 + (np.arange(KB).reshape(1, KB, 1) + rng.random((N, KB, 128))) / KB).reshape(N, KB * 128); k[:, 0, :] = np.cos(a); k[:, 1, :] = np.sin(a)
    for t in range(0, QP, 2):
        j, i = (t // 2) % N, rng.integers(KB * 128); q[ROOT, :2, t] = s[ROOT, t] * k[j, :2, i]; q[ROOT, 3:, t] += k[j, 3:, i] / 8
    return {"q": q.astype(ml_dtypes.bfloat16), "k": k.astype(ml_dtypes.bfloat16), "v": rng.standard_normal((N, 128, KB * 128), dtype=np.float32).astype(ml_dtypes.bfloat16)}
def setup_inputs_big(rng):
    d = setup_inputs(rng)
    for k in ("v",): d[k] = (d[k].astype(np.float32) * 1048576.0).astype(d[k].dtype)
    return d
def setup_inputs_small(rng):
    d = setup_inputs(rng)
    for k in ("v",): d[k] = (d[k].astype(np.float32) * (1 / 1048576.0)).astype(d[k].dtype)
    return d
def reference(q, k, v):
    Q, K, V = q.astype(np.float64), k.astype(np.float64), v.astype(np.float64)
    y = np.full((N, QP, 128), np.nan)
    for r in [ROOT]:
        js = list(range(N))
        S = np.concatenate([K[j].T @ Q[r] for j in js], axis=0)
        P = np.exp(S - S.max(axis=0)); P = P / P.sum(axis=0)
        y[r] = P.T @ np.concatenate([V[j][:, 128 * b:128 * b + 128] for j in js for b in range(KB)], axis=0)
    return {"y": y.astype(ml_dtypes.bfloat16)}

@@ -1,0 +1,220 @@
+from concourse.bass import DstId, RemoteDMATransfer
+from concourse.mybir import AluOpType, AxisListType, ActivationFunctionType
+
+N_RELAYS = 2
+E_RELAY = 8
+E_NEAR = 8
+E_FAR = 8
+E_BACK = 8
+E_KV = 16
+
+W = 40
+QP = 32
+NB = 2
+
+SCRATCH = {
+    "kv": ("sbuf", [128, 512], "bfloat16"),
+    "q4": ("sbuf", [128, 128], "bfloat16"),
+    "vp": ("sbuf", [128, 264], "bfloat16"),
+    "zero": ("sbuf", [128, 8], "float32"),
+    "p": ("sbuf", [128, 64], "bfloat16"),
+    "pt": ("sbuf", [128, 64], "bfloat16"),
+    "land": ("sbuf", [128, 7 * W], "bfloat16"),
+    "ident": ("sbuf", [128, 128], "bfloat16"),
+    "nm": ("sbuf", [128, 1], "float32"),
+    "w": ("sbuf", [128, 8], "float32"),
+    "z": ("sbuf", [128, 7 * 33], "bfloat16"),
+    "r": ("sbuf", [128, 1], "float32"),
+    "yb": ("sbuf", [128, 32], "bfloat16"),
+    "sa": ("psum", [128, 512], "float32"),
+    "sc": ("psum", [128, 512], "float32"),
+    "o": ("psum", [128, 512], "float32"),
+    "acc": ("psum", [128, 512], "float32"),
+}
+SEMAPHORES = ["q", "kv", "loc", "arr", "zr", "vp", "qc", "a", "b", "m", "p", "t", "o", "res",
+              "on", "id", "nm", "w", "acc", "r", "y", "st"] + ["z%d" % j for j in range(7)]
+
+EXP = ActivationFunctionType.Exp
+IDENT = ActivationFunctionType.Identity
+
+
+def _pick(mask, n, avoid=0):
+    bits = [e for e in range(mask.bit_length()) if (mask >> e) & 1]
+    bits.sort(key=lambda e: ((avoid >> e) & 1, e))
+    m = 0
+    for e in bits[:n]:
+        m |= 1 << e
+    return m
+
+
+def _plan(T, topo):
+    cores = list(T.cores)
+    root = cores[T.root]
+    every = range(topo.CHIPS * topo.CORES_PER_CHIP)
+    used = set(cores)
+    worker = []
+    for r in cores:
+        if r == root or (topo.may_write(root, r) and topo.may_write(r, root)):
+            worker.append(r)
+            continue
+        cand = [c for c in every if topo.chip(c) == topo.chip(r) and c not in used and topo.may_write(c, root)]
+        cand.sort(key=lambda c: (topo.die(c) != topo.die(r), c))
+        worker.append(cand[0])
+        used.add(cand[0])
+    near = [x for x in worker if x != root and topo.may_write(root, x)]
+    far = [x for x in worker if x != root and not topo.may_write(root, x)]
+    relays = [c for c in every if topo.chip(c) == topo.chip(root) and c not in used
+              and all(topo.may_write(c, x) for x in far)]
+    relays.sort(key=lambda c: (topo.die(c) != topo.die(root), c))
+    relays = relays[:N_RELAYS] if far else []
+    share = {c: far[i::len(relays)] for i, c in enumerate(relays)}
+    return cores, root, worker, near, far, relays, share
+
+
+def _send_q(g, T, topo, core, dsts, n, avoid=0):
+    mask = topo.mask(core, dsts[0])
+    for d in dsts:
+        mask &= topo.mask(core, d)
+    ids = []
+    for d in dsts:
+        rid, pid, _ = topo.addr(d)
+        ids.append(DstId(rid=rid, pnc=pid))
+    g.remote_dma_fused([RemoteDMATransfer(dst_ids=ids, dma_engine_mask=_pick(mask, n, avoid), remote_sem=T.sem.q,
+                                          srcs=[T.q4[:, 0:QP]], dsts=[T.q4[:, 0:QP] for _ in dsts])],
+                       local_sem=T.sem.loc)
+    return n
+
+
+def _partial(g, T, slot, q_n, kv_n):
+    S = T.sem
+    V, A, P = g.vector, g.scalar, g.tensor
+    negm = T.land[:, W * slot + 33:W * slot + 34]
+    V.memset(T.zero[:], 0.0).then_inc(S.zr, 1)
+    A.wait_ge(S.zr, 1)
+    A.activation(T.vp[:, 32::33], T.zero[:], EXP).then_inc(S.vp, 1)
+    V.wait_ge(S.kv, kv_n)
+    A.wait_ge(S.kv, kv_n)
+    for i in range(4 * NB):
+        dst, src = T.vp[:, 33 * i:33 * i + 32], T.kv[:, 256 + 32 * i:256 + 32 * i + 32]
+        if i % 2 == 0:
+            V.tensor_copy(dst, src).then_inc(S.vp, 1)
+        else:
+            A.activation(dst, src, IDENT).then_inc(S.vp, 1)
+    V.wait_ge(S.q, q_n)
+    A.wait_ge(S.q, q_n)
+    V.tensor_copy(T.q4[:, 32:64], T.q4[:, 0:32]).then_inc(S.qc, 1)
+    A.activation(T.q4[:, 64:96], T.q4[:, 0:32], IDENT).then_inc(S.qc, 1)
+    V.tensor_copy(T.q4[:, 96:128], T.q4[:, 0:32]).then_inc(S.qc, 1)
+    P.wait_ge(S.kv, kv_n)
+    P.wait_ge(S.q, q_n)
+    P.wait_ge(S.qc, 3)
+    P.matmul(T.sa[:, 0:256], T.q4[:], T.kv[:, 0:256], True, True).then_inc(S.a, 1)
+    for c in range(4):
+        for b in range(NB):
+            P.matmul(T.sc[32 * c:32 * c + 32, 32 * b:32 * b + 32], T.q4[:, 0:32],
+                     T.kv[:, 128 * b + 32 * c:128 * b + 32 * c + 32], True, True).then_inc(S.b, 1)
+    V.wait_ge(S.a, 1)
+    V.tensor_reduce(negm, T.sa[:, 0:256], AxisListType.X, AluOpType.max, negate=True).then_inc(S.m, 1)
+    A.wait_ge(S.m, 1)
+    A.wait_ge(S.b, 4 * NB)
+    A.activation(T.p[:], T.sc[:, 0:64], EXP, bias=negm).then_inc(S.p, 1)
+    V.wait_ge(S.p, 1)
+    V.transpose(T.pt[:], T.p[:]).then_inc(S.t, 1)
+    P.wait_ge(S.t, 1)
+    P.wait_ge(S.vp, 1 + 4 * NB)
+    for c in range(4):
+        for b in range(NB):
+            P.matmul(T.o[32 * c:32 * c + 32, 0:33], T.pt[:, 32 * b:32 * b + 32],
+                     T.vp[:, 33 * (4 * b + c):33 * (4 * b + c) + 33], b == 0, b == NB - 1).then_inc(S.o, 1)
+    V.wait_ge(S.o, 4 * NB)
+    V.tensor_copy(T.land[:, W * slot:W * slot + 33], T.o[:, 0:33]).then_inc(S.res, 1)
+
+
+def _load_kv(g, T):
+    g.sync.dma_start(T.kv[:, 0:256], T.k[:]).then_inc(T.sem.kv, 16)
+    g.scalar.dma_start(T.kv[:, 256:512], T.v[:]).then_inc(T.sem.kv, 16)
+    return 32
+
+
+def rank_program(g, core, T, topo):
+    cores, root, worker, near, far, relays, share = _plan(T, topo)
+    S = T.sem
+    n = len(cores)
+
+    if core in share:
+        g.wait_ge(S.q, E_RELAY)
+        g.wait_ge(S.loc, _send_q(g, T, topo, core, share[core], E_FAR))
+        return
+
+    if core in cores and worker[cores.index(core)] != core:
+        x = worker[cores.index(core)]
+        g.wait_ge(S.kv, _load_kv(g, T))
+        rid, pid, _ = topo.addr(x)
+        g.remote_dma(T.kv[:], T.kv[:], S.kv, S.loc, pid, rid, _pick(topo.mask(core, x), E_KV))
+        g.wait_ge(S.loc, E_KV)
+        return
+
+    if core not in worker:
+        return
+    slot = worker.index(core)
+
+    if core != root:
+        kv_n = _load_kv(g, T) if core in cores else E_KV
+        _partial(g, T, slot, E_NEAR if core in near else E_FAR, kv_n)
+        g.wait_ge(S.m, 1)
+        g.wait_ge(S.res, 1)
+        rid, pid, _ = topo.addr(root)
+        part = T.land[:, W * slot:W * slot + 34]
+        g.remote_dma(part, part, S.arr, S.loc, pid, rid, _pick(topo.mask(core, root), E_BACK))
+        g.wait_ge(S.loc, E_BACK)
+        return
+
+    V, A, P = g.vector, g.scalar, g.tensor
+    g.sync.dma_start(T.q4[:, 0:QP], T.q[:]).then_inc(S.q, 16)
+    kv_n = _load_kv(g, T)
+    V.memset(T.ident[:], 1.0).then_inc(S.on, 1)
+    g.wait_ge(S.on, 1)
+    g.affine_select(T.ident[:], T.ident[:], [[-1, 128]], AluOpType.is_equal, 0.0, 0, 1).then_inc(S.id, 1)
+    g.wait_ge(S.q, 16)
+    sent = 0
+    off = 0
+    for d in near:
+        off |= topo.mask(core, d)
+    if relays:
+        sent += _send_q(g, T, topo, core, relays, E_RELAY, avoid=off)
+    if near:
+        sent += _send_q(g, T, topo, core, near, E_NEAR)
+    _partial(g, T, slot, 16, kv_n)
+
+    arr = E_BACK * (n - 1)
+    negms = T.land[:, 33::W]
+    V.wait_ge(S.arr, arr)
+    V.wait_ge(S.m, 1)
+    V.wait_ge(S.res, 1)
+    V.tensor_reduce(T.nm[:], negms, AxisListType.X, AluOpType.min).then_inc(S.nm, 1)
+    A.wait_ge(S.arr, arr)
+    A.wait_ge(S.res, 1)
+    A.wait_ge(S.nm, 1)
+    A.activation(T.w[:, 0:n], negms, EXP, bias=T.nm[:], scale=-1.0).then_inc(S.w, 1)
+    V.wait_ge(S.w, 1)
+    A.wait_ge(S.w, 1)
+    for j in range(n):
+        dst, src, wj = T.z[:, 33 * j:33 * j + 33], T.land[:, W * j:W * j + 33], T.w[:, j:j + 1]
+        if j % 2 == 0:
+            V.tensor_scalar(dst, src, wj, None, AluOpType.mult).then_inc(S["z%d" % j], 1)
+        else:
+            A.activation(dst, src, IDENT, scale=wj).then_inc(S["z%d" % j], 1)
+    P.wait_ge(S.id, 1)
+    for j in range(n):
+        P.wait_ge(S["z%d" % j], 1)
+        P.matmul(T.acc[:, 0:33], T.ident[:], T.z[:, 33 * j:33 * j + 33], j == 0, j == n - 1).then_inc(S.acc, 1)
+    V.wait_ge(S.acc, n)
+    V.reciprocal(T.r[:], T.acc[:, 32:33]).then_inc(S.r, 1)
+    V.wait_ge(S.r, 1)
+    V.tensor_scalar(T.yb[:], T.acc[:, 0:32], T.r[:], None, AluOpType.mult).then_inc(S.y, 1)
+    for c in range(4):
+        qd = g.sync if c % 2 == 0 else g.scalar
+        qd.wait_ge(S.y, 1)
+        qd.dma_start(T.y[:, 32 * c:32 * c + 32], T.yb[32 * c:32 * c + 32, :]).then_inc(S.st, 16)
+    g.wait_ge(S.loc, sent)
+    g.wait_ge(S.st, 64)

@@ -9,6 +9,7 @@ E_BACK = 8
 E_KV = 16
 
 W = 40
+WM = 8
 QP = 32
 NB = 2
 
@@ -20,6 +21,7 @@ SCRATCH = {
     "p": ("sbuf", [128, 64], "bfloat16"),
     "pt": ("sbuf", [128, 64], "bfloat16"),
     "land": ("sbuf", [128, 7 * W], "bfloat16"),
+    "nml": ("sbuf", [128, 7 * WM], "bfloat16"),
     "ident": ("sbuf", [128, 128], "bfloat16"),
     "nm": ("sbuf", [128, 1], "float32"),
     "w": ("sbuf", [128, 8], "float32"),
@@ -31,7 +33,7 @@ SCRATCH = {
     "o": ("psum", [128, 512], "float32"),
     "acc": ("psum", [128, 512], "float32"),
 }
-SEMAPHORES = ["q", "kv", "loc", "arr", "zr", "vp", "qc", "a", "b", "m", "p", "t", "o", "res",
+SEMAPHORES = ["q", "kv", "loc", "arm", "arn", "arf", "zr", "vp", "qc", "a", "b", "m", "p", "t", "o", "res",
               "on", "id", "nm", "w", "acc", "r", "y", "st"] + ["z%d" % j for j in range(7)]
 
 EXP = ActivationFunctionType.Exp
@@ -66,7 +68,7 @@ def _plan(T, topo):
     relays = [c for c in every if topo.chip(c) == topo.chip(root) and c not in used
               and all(topo.may_write(c, x) for x in far)]
     relays.sort(key=lambda c: (topo.die(c) != topo.die(root), c))
-    relays = relays[:N_RELAYS] if far else []
+    relays = relays[:min(N_RELAYS, len(far))]
     share = {c: far[i::len(relays)] for i, c in enumerate(relays)}
     return cores, root, worker, near, far, relays, share
 
@@ -88,7 +90,7 @@ def _send_q(g, T, topo, core, dsts, n, avoid=0):
 def _partial(g, T, slot, q_n, kv_n):
     S = T.sem
     V, A, P = g.vector, g.scalar, g.tensor
-    negm = T.land[:, W * slot + 33:W * slot + 34]
+    negm = T.nml[:, WM * slot:WM * slot + 1]
     V.memset(T.zero[:], 0.0).then_inc(S.zr, 1)
     A.wait_ge(S.zr, 1)
     A.activation(T.vp[:, 32::33], T.zero[:], EXP).then_inc(S.vp, 1)
@@ -161,12 +163,15 @@ def rank_program(g, core, T, topo):
     if core != root:
         kv_n = _load_kv(g, T) if core in cores else E_KV
         _partial(g, T, slot, E_NEAR if core in near else E_FAR, kv_n)
-        g.wait_ge(S.m, 1)
-        g.wait_ge(S.res, 1)
         rid, pid, _ = topo.addr(root)
-        part = T.land[:, W * slot:W * slot + 34]
-        g.remote_dma(part, part, S.arr, S.loc, pid, rid, _pick(topo.mask(core, root), E_BACK))
-        g.wait_ge(S.loc, E_BACK)
+        eng = _pick(topo.mask(core, root), E_BACK)
+        shift = T.nml[:, WM * slot:WM * slot + 1]
+        part = T.land[:, W * slot:W * slot + 33]
+        g.wait_ge(S.m, 1)
+        g.remote_dma(shift, shift, S.arm, S.loc, pid, rid, eng)
+        g.wait_ge(S.res, 1)
+        g.remote_dma(part, part, S.arn if core in near else S.arf, S.loc, pid, rid, eng)
+        g.wait_ge(S.loc, 2 * E_BACK)
         return
 
     V, A, P = g.vector, g.scalar, g.tensor
@@ -186,28 +191,31 @@ def rank_program(g, core, T, topo):
         sent += _send_q(g, T, topo, core, near, E_NEAR)
     _partial(g, T, slot, 16, kv_n)
 
-    arr = E_BACK * (n - 1)
-    negms = T.land[:, 33::W]
-    V.wait_ge(S.arr, arr)
+    negms = T.nml[:, 0::WM]
+    V.wait_ge(S.arm, E_BACK * (n - 1))
     V.wait_ge(S.m, 1)
-    V.wait_ge(S.res, 1)
     V.tensor_reduce(T.nm[:], negms, AxisListType.X, AluOpType.min).then_inc(S.nm, 1)
-    A.wait_ge(S.arr, arr)
-    A.wait_ge(S.res, 1)
+    A.wait_ge(S.arm, E_BACK * (n - 1))
     A.wait_ge(S.nm, 1)
     A.activation(T.w[:, 0:n], negms, EXP, bias=T.nm[:], scale=-1.0).then_inc(S.w, 1)
     V.wait_ge(S.w, 1)
     A.wait_ge(S.w, 1)
-    for j in range(n):
+    order = [slot] + [worker.index(x) for x in near] + [worker.index(x) for x in far]
+    for Q in (V, A):
+        Q.wait_ge(S.res, 1)
+        Q.wait_ge(S.arn, E_BACK * len(near))
+    P.wait_ge(S.id, 1)
+    for i, j in enumerate(order):
+        if i == 1 + len(near):
+            V.wait_ge(S.arf, E_BACK * len(far))
+            A.wait_ge(S.arf, E_BACK * len(far))
         dst, src, wj = T.z[:, 33 * j:33 * j + 33], T.land[:, W * j:W * j + 33], T.w[:, j:j + 1]
-        if j % 2 == 0:
+        if i % 2 == 1:
             V.tensor_scalar(dst, src, wj, None, AluOpType.mult).then_inc(S["z%d" % j], 1)
         else:
             A.activation(dst, src, IDENT, scale=wj).then_inc(S["z%d" % j], 1)
-    P.wait_ge(S.id, 1)
-    for j in range(n):
         P.wait_ge(S["z%d" % j], 1)
-        P.matmul(T.acc[:, 0:33], T.ident[:], T.z[:, 33 * j:33 * j + 33], j == 0, j == n - 1).then_inc(S.acc, 1)
+        P.matmul(T.acc[:, 0:33], T.ident[:], dst, i == 0, i == n - 1).then_inc(S.acc, 1)
     V.wait_ge(S.acc, n)
     V.reciprocal(T.r[:], T.acc[:, 32:33]).then_inc(S.r, 1)
     V.wait_ge(S.r, 1)

@@ -2,7 +2,7 @@ from concourse.bass import DstId, RemoteDMATransfer
 from concourse.mybir import AluOpType, AxisListType, ActivationFunctionType
 
 N_RELAYS = 2
-E_RELAY = 8
+E_RELAY = 4
 E_NEAR = 8
 E_FAR = 8
 E_BACK = 8
@@ -14,18 +14,21 @@ QP = 32
 NB = 2
 
 SCRATCH = {
+    "qd": ("dram", [128, 32], "bfloat16"),
     "kv": ("sbuf", [128, 512], "bfloat16"),
     "q4": ("sbuf", [128, 128], "bfloat16"),
     "vp": ("sbuf", [128, 264], "bfloat16"),
     "zero": ("sbuf", [128, 8], "float32"),
     "p": ("sbuf", [128, 64], "bfloat16"),
     "pt": ("sbuf", [128, 64], "bfloat16"),
-    "land": ("sbuf", [128, 7 * W], "bfloat16"),
-    "nml": ("sbuf", [128, 7 * WM], "bfloat16"),
-    "ident": ("sbuf", [128, 128], "bfloat16"),
+    "land": ("sbuf", [128, 8 * W], "bfloat16"),
+    "nml": ("sbuf", [128, 8 * WM], "bfloat16"),
+    "pmat": ("sbuf", [128, 128], "bfloat16"),
+    "w0": ("sbuf", [128, 8], "float32"),
+    "e": ("sbuf", [128, 3 * W], "float32"),
     "nm": ("sbuf", [128, 1], "float32"),
     "w": ("sbuf", [128, 8], "float32"),
-    "z": ("sbuf", [128, 7 * 33], "bfloat16"),
+    "z": ("sbuf", [128, 5 * 33], "bfloat16"),
     "r": ("sbuf", [128, 1], "float32"),
     "yb": ("sbuf", [128, 32], "bfloat16"),
     "sa": ("psum", [128, 512], "float32"),
@@ -33,8 +36,9 @@ SCRATCH = {
     "o": ("psum", [128, 512], "float32"),
     "acc": ("psum", [128, 512], "float32"),
 }
-SEMAPHORES = ["q", "kv", "loc", "arm", "arn", "arf", "zr", "vp", "qc", "a", "b", "m", "p", "t", "o", "res",
-              "on", "id", "nm", "w", "acc", "r", "y", "st"] + ["z%d" % j for j in range(7)]
+SEMAPHORES = ["q", "qd", "k", "v", "loc", "armn", "armf", "arn", "zr", "vp", "qc", "a", "b", "m", "p", "t", "o",
+              "res", "on", "id", "nm0", "w0", "e", "nm", "w", "acc", "r", "y", "st"] \
+             + ["z%d" % j for j in range(5)] + ["af%d" % j for j in range(4)]
 
 EXP = ActivationFunctionType.Exp
 IDENT = ActivationFunctionType.Identity
@@ -73,7 +77,7 @@ def _plan(T, topo):
     return cores, root, worker, near, far, relays, share
 
 
-def _send_q(g, T, topo, core, dsts, n, avoid=0):
+def _send_q(g, T, topo, core, dsts, n, dst_ap, avoid=0):
     mask = topo.mask(core, dsts[0])
     for d in dsts:
         mask &= topo.mask(core, d)
@@ -82,32 +86,32 @@ def _send_q(g, T, topo, core, dsts, n, avoid=0):
         rid, pid, _ = topo.addr(d)
         ids.append(DstId(rid=rid, pnc=pid))
     g.remote_dma_fused([RemoteDMATransfer(dst_ids=ids, dma_engine_mask=_pick(mask, n, avoid), remote_sem=T.sem.q,
-                                          srcs=[T.q4[:, 0:QP]], dsts=[T.q4[:, 0:QP] for _ in dsts])],
+                                          srcs=[T.qd[:]], dsts=[dst_ap for _ in dsts])],
                        local_sem=T.sem.loc)
     return n
 
 
-def _partial(g, T, slot, q_n, kv_n):
+def _partial(g, T, slot, q_n):
     S = T.sem
     V, A, P = g.vector, g.scalar, g.tensor
     negm = T.nml[:, WM * slot:WM * slot + 1]
     V.memset(T.zero[:], 0.0).then_inc(S.zr, 1)
     A.wait_ge(S.zr, 1)
     A.activation(T.vp[:, 32::33], T.zero[:], EXP).then_inc(S.vp, 1)
-    V.wait_ge(S.kv, kv_n)
-    A.wait_ge(S.kv, kv_n)
-    for i in range(4 * NB):
-        dst, src = T.vp[:, 33 * i:33 * i + 32], T.kv[:, 256 + 32 * i:256 + 32 * i + 32]
-        if i % 2 == 0:
-            V.tensor_copy(dst, src).then_inc(S.vp, 1)
-        else:
-            A.activation(dst, src, IDENT).then_inc(S.vp, 1)
     V.wait_ge(S.q, q_n)
     A.wait_ge(S.q, q_n)
     V.tensor_copy(T.q4[:, 32:64], T.q4[:, 0:32]).then_inc(S.qc, 1)
     A.activation(T.q4[:, 64:96], T.q4[:, 0:32], IDENT).then_inc(S.qc, 1)
     V.tensor_copy(T.q4[:, 96:128], T.q4[:, 0:32]).then_inc(S.qc, 1)
-    P.wait_ge(S.kv, kv_n)
+    V.wait_ge(S.v, 16)
+    A.wait_ge(S.v, 16)
+    for i in range(4 * NB):
+        dst, src = T.vp[:, 33 * i:33 * i + 32], T.kv[:, 256 + 32 * i:256 + 32 * i + 32]
+        if i % 4 == 0:
+            V.tensor_copy(dst, src).then_inc(S.vp, 1)
+        else:
+            A.activation(dst, src, IDENT).then_inc(S.vp, 1)
+    P.wait_ge(S.k, 16)
     P.wait_ge(S.q, q_n)
     P.wait_ge(S.qc, 3)
     P.matmul(T.sa[:, 0:256], T.q4[:], T.kv[:, 0:256], True, True).then_inc(S.a, 1)
@@ -132,97 +136,130 @@ def _partial(g, T, slot, q_n, kv_n):
     V.tensor_copy(T.land[:, W * slot:W * slot + 33], T.o[:, 0:33]).then_inc(S.res, 1)
 
 
-def _load_kv(g, T):
-    g.sync.dma_start(T.kv[:, 0:256], T.k[:]).then_inc(T.sem.kv, 16)
-    g.scalar.dma_start(T.kv[:, 256:512], T.v[:]).then_inc(T.sem.kv, 16)
-    return 32
-
-
 def rank_program(g, core, T, topo):
     cores, root, worker, near, far, relays, share = _plan(T, topo)
     S = T.sem
-    n = len(cores)
+    nf = len(far)
+    slot_of = {x: i for i, x in enumerate(far)}
+    pre = nf
+    early = [root] + near
+    for i, x in enumerate(early):
+        slot_of[x] = nf + 1 + i
 
     if core in share:
         g.wait_ge(S.q, E_RELAY)
-        g.wait_ge(S.loc, _send_q(g, T, topo, core, share[core], E_FAR))
+        g.wait_ge(S.loc, _send_q(g, T, topo, core, share[core], E_FAR, T.q4[:, 0:QP]))
         return
 
     if core in cores and worker[cores.index(core)] != core:
         x = worker[cores.index(core)]
-        g.wait_ge(S.kv, _load_kv(g, T))
+        g.sync.dma_start(T.kv[:, 0:256], T.k[:]).then_inc(S.k, 16)
+        g.sync.dma_start(T.kv[:, 256:512], T.v[:]).then_inc(S.v, 16)
         rid, pid, _ = topo.addr(x)
-        g.remote_dma(T.kv[:], T.kv[:], S.kv, S.loc, pid, rid, _pick(topo.mask(core, x), E_KV))
-        g.wait_ge(S.loc, E_KV)
+        eng = _pick(topo.mask(core, x), E_KV)
+        g.wait_ge(S.k, 16)
+        g.remote_dma(T.kv[:, 0:256], T.kv[:, 0:256], S.k, S.loc, pid, rid, eng)
+        g.wait_ge(S.v, 16)
+        g.remote_dma(T.kv[:, 256:512], T.kv[:, 256:512], S.v, S.loc, pid, rid, eng)
+        g.wait_ge(S.loc, 2 * E_KV)
         return
 
     if core not in worker:
         return
-    slot = worker.index(core)
+    slot = slot_of[core]
 
     if core != root:
-        kv_n = _load_kv(g, T) if core in cores else E_KV
-        _partial(g, T, slot, E_NEAR if core in near else E_FAR, kv_n)
+        if core in cores:
+            g.sync.dma_start(T.kv[:, 0:256], T.k[:]).then_inc(S.k, 16)
+            g.scalar.dma_start(T.kv[:, 256:512], T.v[:]).then_inc(S.v, 16)
+        _partial(g, T, slot, E_NEAR if core in near else E_FAR)
         rid, pid, _ = topo.addr(root)
         eng = _pick(topo.mask(core, root), E_BACK)
         shift = T.nml[:, WM * slot:WM * slot + 1]
         part = T.land[:, W * slot:W * slot + 33]
         g.wait_ge(S.m, 1)
-        g.remote_dma(shift, shift, S.arm, S.loc, pid, rid, eng)
+        g.remote_dma(shift, shift, S.armn if core in near else S.armf, S.loc, pid, rid, eng)
         g.wait_ge(S.res, 1)
-        g.remote_dma(part, part, S.arn if core in near else S.arf, S.loc, pid, rid, eng)
+        g.remote_dma(part, part, S.arn if core in near else S["af%d" % slot], S.loc, pid, rid, eng)
         g.wait_ge(S.loc, 2 * E_BACK)
         return
 
     V, A, P = g.vector, g.scalar, g.tensor
-    g.sync.dma_start(T.q4[:, 0:QP], T.q[:]).then_inc(S.q, 16)
-    kv_n = _load_kv(g, T)
-    V.memset(T.ident[:], 1.0).then_inc(S.on, 1)
+    MUL, ADD, MIN, X = AluOpType.mult, AluOpType.add, AluOpType.min, AxisListType.X
+    g.sync.dma_start(T.qd[:], T.q[:]).then_inc(S.qd, 16)
+    g.scalar.dma_start(T.q4[:, 0:QP], T.q[:]).then_inc(S.q, 16)
+    g.sync.dma_start(T.kv[:, 0:256], T.k[:]).then_inc(S.k, 16)
+    g.scalar.dma_start(T.kv[:, 256:512], T.v[:]).then_inc(S.v, 16)
+    V.memset(T.pmat[:], 1.0).then_inc(S.on, 1)
     g.wait_ge(S.on, 1)
-    g.affine_select(T.ident[:], T.ident[:], [[-1, 128]], AluOpType.is_equal, 0.0, 0, 1).then_inc(S.id, 1)
-    g.wait_ge(S.q, 16)
+    g.affine_select(T.pmat[:], T.pmat[:], [[-1, 32], [-32, 4]],
+                    AluOpType.is_equal, 0.0, 0, 1).then_inc(S.id, 1)
+    g.wait_ge(S.qd, 16)
     sent = 0
     off = 0
     for d in near:
         off |= topo.mask(core, d)
     if relays:
-        sent += _send_q(g, T, topo, core, relays, E_RELAY, avoid=off)
+        sent += _send_q(g, T, topo, core, relays, E_RELAY, T.qd[:], avoid=off)
     if near:
-        sent += _send_q(g, T, topo, core, near, E_NEAR)
-    _partial(g, T, slot, 16, kv_n)
+        sent += _send_q(g, T, topo, core, near, E_NEAR, T.q4[:, 0:QP])
+    _partial(g, T, slot, 16)
 
-    negms = T.nml[:, 0::WM]
-    V.wait_ge(S.arm, E_BACK * (n - 1))
-    V.wait_ge(S.m, 1)
-    V.tensor_reduce(T.nm[:], negms, AxisListType.X, AluOpType.min).then_inc(S.nm, 1)
-    A.wait_ge(S.arm, E_BACK * (n - 1))
-    A.wait_ge(S.nm, 1)
-    A.activation(T.w[:, 0:n], negms, EXP, bias=T.nm[:], scale=-1.0).then_inc(S.w, 1)
-    V.wait_ge(S.w, 1)
-    A.wait_ge(S.w, 1)
-    order = [slot] + [worker.index(x) for x in near] + [worker.index(x) for x in far]
+    ne = len(early)
+    esl = T.nml[:, WM * (nf + 1)::WM]
+    prem = T.nml[:, WM * pre:WM * pre + 1]
     for Q in (V, A):
+        Q.wait_ge(S.armn, E_BACK * len(near))
+        Q.wait_ge(S.m, 1)
+    V.tensor_reduce(prem, esl, X, MIN).then_inc(S.nm0, 1)
+    A.wait_ge(S.nm0, 1)
+    A.activation(T.w0[:, 0:ne], esl, EXP, bias=prem, scale=-1.0).then_inc(S.w0, 1)
+    for Q in (V, A):
+        Q.wait_ge(S.w0, 1)
         Q.wait_ge(S.res, 1)
         Q.wait_ge(S.arn, E_BACK * len(near))
-    P.wait_ge(S.id, 1)
-    for i, j in enumerate(order):
-        if i == 1 + len(near):
-            V.wait_ge(S.arf, E_BACK * len(far))
-            A.wait_ge(S.arf, E_BACK * len(far))
-        dst, src, wj = T.z[:, 33 * j:33 * j + 33], T.land[:, W * j:W * j + 33], T.w[:, j:j + 1]
+    for i in range(ne):
+        j = nf + 1 + i
+        dst, src, wj = T.e[:, W * i:W * i + 33], T.land[:, W * j:W * j + 33], T.w0[:, i:i + 1]
         if i % 2 == 1:
-            V.tensor_scalar(dst, src, wj, None, AluOpType.mult).then_inc(S["z%d" % j], 1)
+            V.tensor_scalar(dst, src, wj, None, MUL).then_inc(S.e, 1)
         else:
-            A.activation(dst, src, IDENT, scale=wj).then_inc(S["z%d" % j], 1)
+            A.activation(dst, src, IDENT, scale=wj).then_inc(S.e, 1)
+    V.wait_ge(S.e, ne)
+    for i in range(1, ne):
+        V.tensor_tensor(T.e[:, 0:33], T.e[:, 0:33], T.e[:, W * i:W * i + 33], ADD).then_inc(S.e, 1)
+        V.wait_ge(S.e, ne + i)
+
+    lsl = T.nml[:, 0:WM * (nf + 1):WM]
+    V.wait_ge(S.nm0, 1)
+    V.wait_ge(S.armf, E_BACK * nf)
+    V.tensor_reduce(T.nm[:], lsl, X, MIN).then_inc(S.nm, 1)
+    A.wait_ge(S.armf, E_BACK * nf)
+    A.wait_ge(S.nm, 1)
+    A.activation(T.w[:, 0:nf + 1], lsl, EXP, bias=T.nm[:], scale=-1.0).then_inc(S.w, 1)
+    V.wait_ge(S.w, 1)
+    A.wait_ge(S.w, 1)
+    P.wait_ge(S.id, 1)
+    order = [pre] + list(range(nf))
+    for i, j in enumerate(order):
+        dst, wj = T.z[:, 33 * j:33 * j + 33], T.w[:, j:j + 1]
+        if j == pre:
+            V.tensor_scalar(dst, T.e[:, 0:33], wj, None, MUL).then_inc(S["z%d" % j], 1)
+        else:
+            src = T.land[:, W * j:W * j + 33]
+            if j % 2 == 0:
+                V.wait_ge(S["af%d" % j], E_BACK)
+                V.tensor_scalar(dst, src, wj, None, MUL).then_inc(S["z%d" % j], 1)
+            else:
+                A.wait_ge(S["af%d" % j], E_BACK)
+                A.activation(dst, src, IDENT, scale=wj).then_inc(S["z%d" % j], 1)
         P.wait_ge(S["z%d" % j], 1)
-        P.matmul(T.acc[:, 0:33], T.ident[:], dst, i == 0, i == n - 1).then_inc(S.acc, 1)
-    V.wait_ge(S.acc, n)
+        P.matmul(T.acc[:, 0:33], T.pmat[:], dst, i == 0, i == len(order) - 1).then_inc(S.acc, 1)
+    V.wait_ge(S.acc, len(order))
     V.reciprocal(T.r[:], T.acc[:, 32:33]).then_inc(S.r, 1)
     V.wait_ge(S.r, 1)
-    V.tensor_scalar(T.yb[:], T.acc[:, 0:32], T.r[:], None, AluOpType.mult).then_inc(S.y, 1)
-    for c in range(4):
-        qd = g.sync if c % 2 == 0 else g.scalar
-        qd.wait_ge(S.y, 1)
-        qd.dma_start(T.y[:, 32 * c:32 * c + 32], T.yb[32 * c:32 * c + 32, :]).then_inc(S.st, 16)
+    V.tensor_scalar(T.yb[:], T.acc[:, 0:32], T.r[:], None, MUL).then_inc(S.y, 1)
+    g.sync.wait_ge(S.y, 1)
+    g.sync.dma_start(T.y[:], T.yb[:]).then_inc(S.st, 16)
     g.wait_ge(S.loc, sent)
-    g.wait_ge(S.st, 64)
+    g.wait_ge(S.st, 16)

from concourse.bass import DstId, RemoteDMATransfer
from concourse.mybir import AluOpType, AxisListType, ActivationFunctionType

N_RELAYS = 2
E_RELAY = 4
E_NEAR = 8
E_FAR = 8
E_BACK = 8
E_KV = 16

W = 40
WM = 8
QP = 32
NB = 2

SCRATCH = {
    "qd": ("dram", [128, 32], "bfloat16"),
    "kv": ("sbuf", [128, 512], "bfloat16"),
    "q4": ("sbuf", [128, 128], "bfloat16"),
    "vp": ("sbuf", [128, 264], "bfloat16"),
    "zero": ("sbuf", [128, 8], "float32"),
    "p": ("sbuf", [128, 64], "bfloat16"),
    "pt": ("sbuf", [128, 64], "bfloat16"),
    "land": ("sbuf", [128, 8 * W], "bfloat16"),
    "nml": ("sbuf", [128, 8 * WM], "bfloat16"),
    "pmat": ("sbuf", [128, 128], "bfloat16"),
    "w0": ("sbuf", [128, 8], "float32"),
    "e": ("sbuf", [128, 3 * W], "float32"),
    "nm": ("sbuf", [128, 1], "float32"),
    "w": ("sbuf", [128, 8], "float32"),
    "z": ("sbuf", [128, 5 * 33], "bfloat16"),
    "r": ("sbuf", [128, 1], "float32"),
    "yb": ("sbuf", [128, 32], "bfloat16"),
    "sa": ("psum", [128, 512], "float32"),
    "sc": ("psum", [128, 512], "float32"),
    "o": ("psum", [128, 512], "float32"),
    "acc": ("psum", [128, 512], "float32"),
}
SEMAPHORES = ["q", "qd", "k", "v", "loc", "armn", "armf", "arn", "zr", "vp", "qc", "a", "b", "m", "p", "t", "o",
              "res", "on", "id", "nm0", "w0", "e", "nm", "w", "acc", "r", "y", "st"] \
             + ["z%d" % j for j in range(5)] + ["af%d" % j for j in range(4)]

EXP = ActivationFunctionType.Exp
IDENT = ActivationFunctionType.Identity


def _pick(mask, n, avoid=0):
    bits = [e for e in range(mask.bit_length()) if (mask >> e) & 1]
    bits.sort(key=lambda e: ((avoid >> e) & 1, e))
    m = 0
    for e in bits[:n]:
        m |= 1 << e
    return m


def _plan(T, topo):
    cores = list(T.cores)
    root = cores[T.root]
    every = range(topo.CHIPS * topo.CORES_PER_CHIP)
    used = set(cores)
    worker = []
    for r in cores:
        if r == root or (topo.may_write(root, r) and topo.may_write(r, root)):
            worker.append(r)
            continue
        cand = [c for c in every if topo.chip(c) == topo.chip(r) and c not in used and topo.may_write(c, root)]
        cand.sort(key=lambda c: (topo.die(c) != topo.die(r), c))
        worker.append(cand[0])
        used.add(cand[0])
    near = [x for x in worker if x != root and topo.may_write(root, x)]
    far = [x for x in worker if x != root and not topo.may_write(root, x)]
    relays = [c for c in every if topo.chip(c) == topo.chip(root) and c not in used
              and all(topo.may_write(c, x) for x in far)]
    relays.sort(key=lambda c: (topo.die(c) != topo.die(root), c))
    relays = relays[:min(N_RELAYS, len(far))]
    share = {c: far[i::len(relays)] for i, c in enumerate(relays)}
    return cores, root, worker, near, far, relays, share


def _send_q(g, T, topo, core, dsts, n, dst_ap, avoid=0):
    mask = topo.mask(core, dsts[0])
    for d in dsts:
        mask &= topo.mask(core, d)
    ids = []
    for d in dsts:
        rid, pid, _ = topo.addr(d)
        ids.append(DstId(rid=rid, pnc=pid))
    g.remote_dma_fused([RemoteDMATransfer(dst_ids=ids, dma_engine_mask=_pick(mask, n, avoid), remote_sem=T.sem.q,
                                          srcs=[T.qd[:]], dsts=[dst_ap for _ in dsts])],
                       local_sem=T.sem.loc)
    return n


def _partial(g, T, slot, q_n):
    S = T.sem
    V, A, P = g.vector, g.scalar, g.tensor
    negm = T.nml[:, WM * slot:WM * slot + 1]
    V.memset(T.zero[:], 0.0).then_inc(S.zr, 1)
    A.wait_ge(S.zr, 1)
    A.activation(T.vp[:, 32::33], T.zero[:], EXP).then_inc(S.vp, 1)
    V.wait_ge(S.q, q_n)
    A.wait_ge(S.q, q_n)
    V.tensor_copy(T.q4[:, 32:64], T.q4[:, 0:32]).then_inc(S.qc, 1)
    A.activation(T.q4[:, 64:96], T.q4[:, 0:32], IDENT).then_inc(S.qc, 1)
    V.tensor_copy(T.q4[:, 96:128], T.q4[:, 0:32]).then_inc(S.qc, 1)
    V.wait_ge(S.v, 16)
    A.wait_ge(S.v, 16)
    for i in range(4 * NB):
        dst, src = T.vp[:, 33 * i:33 * i + 32], T.kv[:, 256 + 32 * i:256 + 32 * i + 32]
        if i % 4 == 0:
            V.tensor_copy(dst, src).then_inc(S.vp, 1)
        else:
            A.activation(dst, src, IDENT).then_inc(S.vp, 1)
    P.wait_ge(S.k, 16)
    P.wait_ge(S.q, q_n)
    P.wait_ge(S.qc, 3)
    P.matmul(T.sa[:, 0:256], T.q4[:], T.kv[:, 0:256], True, True).then_inc(S.a, 1)
    for c in range(4):
        for b in range(NB):
            P.matmul(T.sc[32 * c:32 * c + 32, 32 * b:32 * b + 32], T.q4[:, 0:32],
                     T.kv[:, 128 * b + 32 * c:128 * b + 32 * c + 32], True, True).then_inc(S.b, 1)
    V.wait_ge(S.a, 1)
    V.tensor_reduce(negm, T.sa[:, 0:256], AxisListType.X, AluOpType.max, negate=True).then_inc(S.m, 1)
    A.wait_ge(S.m, 1)
    A.wait_ge(S.b, 4 * NB)
    A.activation(T.p[:], T.sc[:, 0:64], EXP, bias=negm).then_inc(S.p, 1)
    V.wait_ge(S.p, 1)
    V.transpose(T.pt[:], T.p[:]).then_inc(S.t, 1)
    P.wait_ge(S.t, 1)
    P.wait_ge(S.vp, 1 + 4 * NB)
    for c in range(4):
        for b in range(NB):
            P.matmul(T.o[32 * c:32 * c + 32, 0:33], T.pt[:, 32 * b:32 * b + 32],
                     T.vp[:, 33 * (4 * b + c):33 * (4 * b + c) + 33], b == 0, b == NB - 1).then_inc(S.o, 1)
    V.wait_ge(S.o, 4 * NB)
    V.tensor_copy(T.land[:, W * slot:W * slot + 33], T.o[:, 0:33]).then_inc(S.res, 1)


def rank_program(g, core, T, topo):
    cores, root, worker, near, far, relays, share = _plan(T, topo)
    S = T.sem
    nf = len(far)
    slot_of = {x: i for i, x in enumerate(far)}
    pre = nf
    early = [root] + near
    for i, x in enumerate(early):
        slot_of[x] = nf + 1 + i

    if core in share:
        g.wait_ge(S.q, E_RELAY)
        g.wait_ge(S.loc, _send_q(g, T, topo, core, share[core], E_FAR, T.q4[:, 0:QP]))
        return

    if core in cores and worker[cores.index(core)] != core:
        x = worker[cores.index(core)]
        g.sync.dma_start(T.kv[:, 0:256], T.k[:]).then_inc(S.k, 16)
        g.sync.dma_start(T.kv[:, 256:512], T.v[:]).then_inc(S.v, 16)
        rid, pid, _ = topo.addr(x)
        eng = _pick(topo.mask(core, x), E_KV)
        g.wait_ge(S.k, 16)
        g.remote_dma(T.kv[:, 0:256], T.kv[:, 0:256], S.k, S.loc, pid, rid, eng)
        g.wait_ge(S.v, 16)
        g.remote_dma(T.kv[:, 256:512], T.kv[:, 256:512], S.v, S.loc, pid, rid, eng)
        g.wait_ge(S.loc, 2 * E_KV)
        return

    if core not in worker:
        return
    slot = slot_of[core]

    if core != root:
        if core in cores:
            g.sync.dma_start(T.kv[:, 0:256], T.k[:]).then_inc(S.k, 16)
            g.scalar.dma_start(T.kv[:, 256:512], T.v[:]).then_inc(S.v, 16)
        _partial(g, T, slot, E_NEAR if core in near else E_FAR)
        rid, pid, _ = topo.addr(root)
        eng = _pick(topo.mask(core, root), E_BACK)
        shift = T.nml[:, WM * slot:WM * slot + 1]
        part = T.land[:, W * slot:W * slot + 33]
        g.wait_ge(S.m, 1)
        g.remote_dma(shift, shift, S.armn if core in near else S.armf, S.loc, pid, rid, eng)
        g.wait_ge(S.res, 1)
        g.remote_dma(part, part, S.arn if core in near else S["af%d" % slot], S.loc, pid, rid, eng)
        g.wait_ge(S.loc, 2 * E_BACK)
        return

    V, A, P = g.vector, g.scalar, g.tensor
    MUL, ADD, MIN, X = AluOpType.mult, AluOpType.add, AluOpType.min, AxisListType.X
    g.sync.dma_start(T.qd[:], T.q[:]).then_inc(S.qd, 16)
    g.scalar.dma_start(T.q4[:, 0:QP], T.q[:]).then_inc(S.q, 16)
    g.sync.dma_start(T.kv[:, 0:256], T.k[:]).then_inc(S.k, 16)
    g.scalar.dma_start(T.kv[:, 256:512], T.v[:]).then_inc(S.v, 16)
    V.memset(T.pmat[:], 1.0).then_inc(S.on, 1)
    g.wait_ge(S.on, 1)
    g.affine_select(T.pmat[:], T.pmat[:], [[-1, 32], [-32, 4]],
                    AluOpType.is_equal, 0.0, 0, 1).then_inc(S.id, 1)
    g.wait_ge(S.qd, 16)
    sent = 0
    off = 0
    for d in near:
        off |= topo.mask(core, d)
    if relays:
        sent += _send_q(g, T, topo, core, relays, E_RELAY, T.qd[:], avoid=off)
    if near:
        sent += _send_q(g, T, topo, core, near, E_NEAR, T.q4[:, 0:QP])
    _partial(g, T, slot, 16)

    ne = len(early)
    esl = T.nml[:, WM * (nf + 1)::WM]
    prem = T.nml[:, WM * pre:WM * pre + 1]
    for Q in (V, A):
        Q.wait_ge(S.armn, E_BACK * len(near))
        Q.wait_ge(S.m, 1)
    V.tensor_reduce(prem, esl, X, MIN).then_inc(S.nm0, 1)
    A.wait_ge(S.nm0, 1)
    A.activation(T.w0[:, 0:ne], esl, EXP, bias=prem, scale=-1.0).then_inc(S.w0, 1)
    for Q in (V, A):
        Q.wait_ge(S.w0, 1)
        Q.wait_ge(S.res, 1)
        Q.wait_ge(S.arn, E_BACK * len(near))
    for i in range(ne):
        j = nf + 1 + i
        dst, src, wj = T.e[:, W * i:W * i + 33], T.land[:, W * j:W * j + 33], T.w0[:, i:i + 1]
        if i % 2 == 1:
            V.tensor_scalar(dst, src, wj, None, MUL).then_inc(S.e, 1)
        else:
            A.activation(dst, src, IDENT, scale=wj).then_inc(S.e, 1)
    V.wait_ge(S.e, ne)
    for i in range(1, ne):
        V.tensor_tensor(T.e[:, 0:33], T.e[:, 0:33], T.e[:, W * i:W * i + 33], ADD).then_inc(S.e, 1)
        V.wait_ge(S.e, ne + i)

    lsl = T.nml[:, 0:WM * (nf + 1):WM]
    V.wait_ge(S.nm0, 1)
    V.wait_ge(S.armf, E_BACK * nf)
    V.tensor_reduce(T.nm[:], lsl, X, MIN).then_inc(S.nm, 1)
    A.wait_ge(S.armf, E_BACK * nf)
    A.wait_ge(S.nm, 1)
    A.activation(T.w[:, 0:nf + 1], lsl, EXP, bias=T.nm[:], scale=-1.0).then_inc(S.w, 1)
    V.wait_ge(S.w, 1)
    A.wait_ge(S.w, 1)
    P.wait_ge(S.id, 1)
    order = [pre] + list(range(nf))
    for i, j in enumerate(order):
        dst, wj = T.z[:, 33 * j:33 * j + 33], T.w[:, j:j + 1]
        if j == pre:
            V.tensor_scalar(dst, T.e[:, 0:33], wj, None, MUL).then_inc(S["z%d" % j], 1)
        else:
            src = T.land[:, W * j:W * j + 33]
            if j % 2 == 0:
                V.wait_ge(S["af%d" % j], E_BACK)
                V.tensor_scalar(dst, src, wj, None, MUL).then_inc(S["z%d" % j], 1)
            else:
                A.wait_ge(S["af%d" % j], E_BACK)
                A.activation(dst, src, IDENT, scale=wj).then_inc(S["z%d" % j], 1)
        P.wait_ge(S["z%d" % j], 1)
        P.matmul(T.acc[:, 0:33], T.pmat[:], dst, i == 0, i == len(order) - 1).then_inc(S.acc, 1)
    V.wait_ge(S.acc, len(order))
    V.reciprocal(T.r[:], T.acc[:, 32:33]).then_inc(S.r, 1)
    V.wait_ge(S.r, 1)
    V.tensor_scalar(T.yb[:], T.acc[:, 0:32], T.r[:], None, MUL).then_inc(S.y, 1)
    g.sync.wait_ge(S.y, 1)
    g.sync.dma_start(T.y[:], T.yb[:]).then_inc(S.st, 16)
    g.wait_ge(S.loc, sent)
    g.wait_ge(S.st, 16)
